import numpy as np
import ml_dtypes


def mxq(x, axis, fmt="e4m3"):
    dtype, down = {"e4m3": (ml_dtypes.float8_e4m3fn, 7), "e5m2": (ml_dtypes.float8_e5m2, 14)}[fmt]
    v = np.moveaxis(np.asarray(x, np.float32).astype(ml_dtypes.bfloat16).astype(np.float64), axis, -1)
    blocks = v.reshape(v.shape[:-1] + (-1, 32))
    amax = np.abs(blocks).max(-1, keepdims=True)
    byte = np.maximum(np.where(amax > 0, np.frexp(amax)[1] - 1 + 127, 0) - down, 1)
    scale = np.exp2(byte - 127.0)
    codes = (blocks / scale).astype(np.float32).astype(dtype).astype(np.float64)
    return np.moveaxis((codes * scale).reshape(v.shape), -1, axis)


WIDE = False


def mx_kscale(k):
    if not WIDE:
        return np.ones(k)
    levels = np.array([10, -10, 5, -5, 0])
    if k % 512:
        return np.exp2(np.random.permutation(np.resize(levels, k // 32))).repeat(32)
    a = np.empty((k // 512, 16))
    for p in range(k // 512):
        a[p, :8] = np.random.permutation(np.resize(levels, 8))
        for g in range(8):
            far = levels[np.abs(levels - a[p, g]) >= 10]
            a[p, g + 8] = far[np.random.randint(len(far))]
    return np.exp2(a.ravel()).repeat(32)


def f64(x):
    return np.asarray(x).astype(np.float64)


def striped(idx):
    return np.tile(idx.reshape(-1, 16).T, (8, 1)).astype(np.uint16)


def unstriped(offs):
    return offs[:16].T.reshape(-1).astype(np.int64)


E2M1 = np.array([0.0, 0.5, 1.0, 1.5, 2.0, 3.0, 4.0, 6.0, -0.0, -0.5, -1.0, -1.5, -2.0, -3.0, -4.0, -6.0])


def pack_fp4(w):
    k, n = w.shape
    w = f64(np.asarray(w, np.float32).astype(ml_dtypes.bfloat16)).reshape(k // 32, 32, n)
    amax = np.abs(w).max(1)
    mant, ex = np.frexp(amax / 6.0)
    byte = np.clip(np.where(amax > 0, np.where(mant > 0.5, ex, ex - 1) + 127, 1), 1, 254)
    scaled = (w * np.exp2(127.0 - byte)[:, None, :]).reshape(k, n).astype(np.float32)
    c = np.ascontiguousarray(scaled.reshape(k // 512, 128, 4, n).transpose(0, 1, 3, 2)).astype(ml_dtypes.float4_e2m1fn).view(np.uint8) & 0xF
    words = (c[..., 0::2] | (c[..., 1::2] << 4)).reshape(k // 512, 128, 2 * n)
    return np.ascontiguousarray(words), np.ascontiguousarray(byte.astype(np.uint8).reshape(k // 512, 16, n))


def unpack_fp4(words, scales):
    g, _, n = scales.shape
    words = np.ascontiguousarray(words).reshape(g, 128, n, 2)
    nib = np.empty((g, 128, n, 4), np.uint8)
    nib[..., 0::2] = words & 0xF
    nib[..., 1::2] = words >> 4
    vals = E2M1[nib] * np.repeat(np.exp2(scales.astype(np.float64) - 127.0), 8, axis=1)[..., None]
    return vals.transpose(0, 1, 3, 2).reshape(g * 512, n)


def sigmoid(v):
    return 1.0 / (1.0 + np.exp(-np.maximum(v, -700.0)))


K, T, N, U = 1024, 512, 256, 1024


def setup_inputs():
    n = np.random.standard_normal
    s = mx_kscale(K)[:, None]
    packed_xT = pack_fp4(n((K, T)) * s)
    return {
        "x_words": packed_xT[0],
        "x_scales": packed_xT[1],
        "mem": n((N, U)).astype(np.float32),
        "w1": (n((K, N)) / np.sqrt(K) / s).astype(np.float32),
        "slot": striped(np.random.permutation(U)[:T]),
    }


def reference(x_words, x_scales, mem, w1, slot):
    xq = unpack_fp4(x_words, x_scales)
    y = mxq(f64(w1), 0, "e4m3").T @ xq
    out = f64(mem).copy()
    out[:, unstriped(slot)] = f64(mem)[:, unstriped(slot)] * sigmoid(y)
    return out

@@ -1,0 +1,112 @@
+from contextlib import ExitStack
+
+import concourse.mybir as mybir
+
+K, T, N, U = 1024, 512, 256, 1024
+FLOPS = 2 * K * T * N
+
+F32 = mybir.dt.float32
+BF16 = mybir.dt.bfloat16
+I32 = mybir.dt.int32
+U32 = mybir.dt.uint32
+U16 = mybir.dt.uint16
+U8 = mybir.dt.uint8
+FP8X4 = mybir.dt.float8_e4m3fn_x4
+FP4X4 = mybir.dt.float4_e2m1fn_x4
+MULT = mybir.AluOpType.mult
+SIGMOID = mybir.ActivationFunctionType.Sigmoid
+
+P = 128
+PACK = 4
+K_PASS = P * PACK
+PASSES = K // K_PASS
+SPLIT = 384
+
+
+def tile_picked_widxput_gate_l_kernel(tc, x_words, x_scales, mem, w1, slot, out):
+    nc = tc.nc
+    with ExitStack() as ctx:
+        keep = ctx.enter_context(tc.tile_pool(name="keep", bufs=1))
+        psum = ctx.enter_context(tc.psum_pool(name="psum", bufs=1))
+
+        offsets = keep.tile([P, T // 16], U16, name="offsets")
+        xw = keep.tile([P, PASSES, 2 * T], U8, name="xw", align_bytes=64)
+        xs = keep.tile([P, PASSES, T], U8, name="xs", align_bytes=64)
+        raw0 = [keep.tile([P, PACK, P], F32, name=f"raw0{z}") for z in range(PASSES)]
+        raw1 = keep.tile([P, PASSES * PACK * P], F32, name="raw1")
+        grouped0 = [keep.tile([P, P * PACK], BF16, name=f"grouped0{z}", align_bytes=64) for z in range(PASSES)]
+        grouped1 = keep.tile([P, PASSES * P * PACK], BF16, name="grouped1", align_bytes=64)
+        codes0 = [keep.tile([P, P], U32, name=f"codes0{z}", align_bytes=64) for z in range(PASSES)]
+        scales0 = [keep.tile([P, P], U8, name=f"scales0{z}", align_bytes=64) for z in range(PASSES)]
+        codes1 = keep.tile([P, PASSES * P], U32, name="codes1", align_bytes=64)
+        scales1 = keep.tile([P, PASSES * P], U8, name="scales1", align_bytes=64)
+        store = [keep.tile([P, U], F32, name=f"store{b}") for b in range(2)]
+        old0 = keep.tile([P, T], F32, name="old0")
+        gate0a = keep.tile([P, SPLIT], F32, name="gate0a")
+        gate1 = keep.tile([P, T], F32, name="gate1")
+        acc = [psum.tile([P, T], F32, name=f"acc{b}") for b in range(2)]
+
+        def w_rows(b, z):
+            rows = w1[z * K_PASS : (z + 1) * K_PASS, b * P : (b + 1) * P]
+            return rows.rearrange("(p j) m -> p j m", j=PACK)
+
+        def project(b, codes, scales):
+            for z in range(PASSES):
+                nc.tensor.matmul_mx(
+                    out=acc[b][:],
+                    lhsT=codes[z].bitcast(FP8X4),
+                    lhsT_scale=scales[z],
+                    rhs=xw[:, z, :].bitcast(FP4X4),
+                    rhs_scale=xs[:, z, :],
+                    start=(z == 0),
+                    stop=(z == PASSES - 1),
+                )
+
+        def scatter(b, lo, hi, old, gate):
+            nc.vector.tensor_tensor(store[b][:].indirect(offsets[:, lo // 16 : hi // 16]), old, gate, MULT)
+
+        scale_rows = x_scales.rearrange("z (q r) c -> r q z c", r=4)
+        for r in range(4):
+            nc.scalar.dma_start(out=xs[r:P:32, :, :].bitcast(I32), in_=scale_rows[r].bitcast(I32))
+        for z in range(PASSES):
+            nc.sync.dma_start(out=raw0[z][:], in_=w_rows(0, z))
+        nc.sync.dma_start(out=xw[:].bitcast(I32), in_=x_words.rearrange("z p c -> p z c").bitcast(I32))
+        nc.sync.dma_start(offsets[:], slot)
+        nc.sync.dma_start(out=store[0][:], in_=mem[0:P, :])
+        for z in range(PASSES):
+            nc.sync.dma_start(
+                out=raw1[:, z * K_PASS : (z + 1) * K_PASS].rearrange("p (j m) -> p j m", j=PACK), in_=w_rows(1, z)
+            )
+        nc.sync.dma_start(out=store[1][:], in_=mem[P : 2 * P, :])
+
+        for z in range(PASSES):
+            nc.vector.tensor_copy(
+                out=grouped0[z][:].rearrange("p (c i j) -> p c j i", i=4, j=PACK),
+                in_=raw0[z][:].rearrange("p j (c i) -> p c j i", i=4),
+            )
+        for z in range(PASSES):
+            nc.vector.quantize_mx(out=codes0[z][:].bitcast(FP8X4), scales=scales0[z][:], in_=grouped0[z][:])
+        project(0, [t[:] for t in codes0], [t[:] for t in scales0])
+        nc.scalar.activation(out=gate0a[:], in_=acc[0][:, 0:SPLIT], func=SIGMOID)
+        nc.vector.tensor_copy(old0[:], store[0][:].indirect(offsets[:]))
+        scatter(0, 0, SPLIT, old0[:, 0:SPLIT], gate0a[:])
+
+        nc.scalar.copy(
+            out=grouped1[:].rearrange("p (z c i j) -> p z c j i", z=PASSES, i=4, j=PACK),
+            in_=raw1[:].rearrange("p (z j c i) -> p z c j i", z=PASSES, j=PACK, i=4),
+        )
+        gate0b = raw1[:, 0 : T - SPLIT]
+        old1 = raw1[:, T : 2 * T]
+        nc.scalar.activation(out=gate0b, in_=acc[0][:, SPLIT:T], func=SIGMOID)
+        nc.vector.quantize_mx(out=codes1[:].bitcast(FP8X4), scales=scales1[:], in_=grouped1[:])
+        project(
+            1,
+            [codes1[:, z * P : (z + 1) * P] for z in range(PASSES)],
+            [scales1[:, z * P : (z + 1) * P] for z in range(PASSES)],
+        )
+        nc.scalar.activation(out=gate1[:], in_=acc[1][:], func=SIGMOID)
+        nc.vector.tensor_copy(old1, store[1][:].indirect(offsets[:]))
+        scatter(0, SPLIT, T, old0[:, SPLIT:T], gate0b)
+        nc.sync.dma_start(out=out[0:P, :], in_=store[0][:])
+        scatter(1, 0, T, old1, gate1[:])
+        nc.sync.dma_start(out=out[P : 2 * P, :], in_=store[1][:])

@@ -20,7 +20,7 @@ P = 128
 PACK = 4
 K_PASS = P * PACK
 PASSES = K // K_PASS
-SPLIT = 384
+SPLIT = 256
 
 
 def tile_picked_widxput_gate_l_kernel(tc, x_words, x_scales, mem, w1, slot, out):
@@ -44,20 +44,22 @@ def tile_picked_widxput_gate_l_kernel(tc, x_words, x_scales, mem, w1, slot, out)
         old0 = keep.tile([P, T], F32, name="old0")
         gate0a = keep.tile([P, SPLIT], F32, name="gate0a")
         gate1 = keep.tile([P, T], F32, name="gate1")
-        acc = [psum.tile([P, T], F32, name=f"acc{b}") for b in range(2)]
+        acc0a = psum.tile([P, SPLIT], F32, name="acc0a")
+        acc0b = psum.tile([P, T - SPLIT], F32, name="acc0b")
+        acc1 = psum.tile([P, T], F32, name="acc1")
 
         def w_rows(b, z):
             rows = w1[z * K_PASS : (z + 1) * K_PASS, b * P : (b + 1) * P]
             return rows.rearrange("(p j) m -> p j m", j=PACK)
 
-        def project(b, codes, scales):
+        def project(acc, lo, hi, codes, scales):
             for z in range(PASSES):
                 nc.tensor.matmul_mx(
-                    out=acc[b][:],
+                    out=acc,
                     lhsT=codes[z].bitcast(FP8X4),
                     lhsT_scale=scales[z],
-                    rhs=xw[:, z, :].bitcast(FP4X4),
-                    rhs_scale=xs[:, z, :],
+                    rhs=xw[:, z, 2 * lo : 2 * hi].bitcast(FP4X4),
+                    rhs_scale=xs[:, z, lo:hi],
                     start=(z == 0),
                     stop=(z == PASSES - 1),
                 )
@@ -66,13 +68,15 @@ def tile_picked_widxput_gate_l_kernel(tc, x_words, x_scales, mem, w1, slot, out)
             nc.vector.tensor_tensor(store[b][:].indirect(offsets[:, lo // 16 : hi // 16]), old, gate, MULT)
 
         scale_rows = x_scales.rearrange("z (q r) c -> r q z c", r=4)
+        nc.sync.dma_start(out=raw0[0][:], in_=w_rows(0, 0))
         for r in range(4):
-            nc.scalar.dma_start(out=xs[r:P:32, :, :].bitcast(I32), in_=scale_rows[r].bitcast(I32))
-        for z in range(PASSES):
-            nc.sync.dma_start(out=raw0[z][:], in_=w_rows(0, z))
-        nc.sync.dma_start(out=xw[:].bitcast(I32), in_=x_words.rearrange("z p c -> p z c").bitcast(I32))
-        nc.sync.dma_start(offsets[:], slot)
+            nc.sync.dma_start(out=xs[r:P:32, :, :].bitcast(I32), in_=scale_rows[r].bitcast(I32))
+        nc.sync.dma_start(out=raw0[1][:], in_=w_rows(0, 1))
+        x_cols = x_words.rearrange("z p c -> p z c")
+        nc.sync.dma_start(out=xw[:, :, 0:2 * SPLIT].bitcast(I32), in_=x_cols[:, :, 0:2 * SPLIT].bitcast(I32))
         nc.sync.dma_start(out=store[0][:], in_=mem[0:P, :])
+        nc.sync.dma_start(offsets[:], slot)
+        nc.sync.dma_start(out=xw[:, :, 2 * SPLIT:2 * T].bitcast(I32), in_=x_cols[:, :, 2 * SPLIT:2 * T].bitcast(I32))
         for z in range(PASSES):
             nc.sync.dma_start(
                 out=raw1[:, z * K_PASS : (z + 1) * K_PASS].rearrange("p (j m) -> p j m", j=PACK), in_=w_rows(1, z)
@@ -86,25 +90,32 @@ def tile_picked_widxput_gate_l_kernel(tc, x_words, x_scales, mem, w1, slot, out)
             )
         for z in range(PASSES):
             nc.vector.quantize_mx(out=codes0[z][:].bitcast(FP8X4), scales=scales0[z][:], in_=grouped0[z][:])
-        project(0, [t[:] for t in codes0], [t[:] for t in scales0])
-        nc.scalar.activation(out=gate0a[:], in_=acc[0][:, 0:SPLIT], func=SIGMOID)
+        for lo in range(0, SPLIT, P):
+            project(acc0a[:, lo : lo + P], lo, lo + P, [t[:] for t in codes0], [t[:] for t in scales0])
+        for lo in range(SPLIT, T, P):
+            project(acc0b[:, lo - SPLIT : lo - SPLIT + P], lo, lo + P, [t[:] for t in codes0], [t[:] for t in scales0])
+        nc.scalar.activation(out=gate0a[:], in_=acc0a[:], func=SIGMOID)
         nc.vector.tensor_copy(old0[:], store[0][:].indirect(offsets[:]))
         scatter(0, 0, SPLIT, old0[:, 0:SPLIT], gate0a[:])
 
-        nc.scalar.copy(
-            out=grouped1[:].rearrange("p (z c i j) -> p z c j i", z=PASSES, i=4, j=PACK),
-            in_=raw1[:].rearrange("p (z j c i) -> p z c j i", z=PASSES, j=PACK, i=4),
-        )
-        gate0b = raw1[:, 0 : T - SPLIT]
-        old1 = raw1[:, T : 2 * T]
-        nc.scalar.activation(out=gate0b, in_=acc[0][:, SPLIT:T], func=SIGMOID)
+        for z in range(PASSES):
+            cols = slice(z * K_PASS, (z + 1) * K_PASS)
+            nc.scalar.copy(
+                out=grouped1[:, cols].rearrange("p (c i j) -> p c j i", i=4, j=PACK),
+                in_=raw1[:, cols].rearrange("p (j c i) -> p c j i", j=PACK, i=4),
+            )
+        old1 = raw1[:, SPLIT : SPLIT + T]
+        gate0b = raw1[:, SPLIT + T : 2 * T]
+        nc.scalar.activation(out=gate0b, in_=acc0b[:], func=SIGMOID)
         nc.vector.quantize_mx(out=codes1[:].bitcast(FP8X4), scales=scales1[:], in_=grouped1[:])
         project(
-            1,
+            acc1[:],
+            0,
+            T,
             [codes1[:, z * P : (z + 1) * P] for z in range(PASSES)],
             [scales1[:, z * P : (z + 1) * P] for z in range(PASSES)],
         )
-        nc.scalar.activation(out=gate1[:], in_=acc[1][:], func=SIGMOID)
+        nc.scalar.activation(out=gate1[:], in_=acc1[:], func=SIGMOID)
         nc.vector.tensor_copy(old1, store[1][:].indirect(offsets[:]))
         scatter(0, SPLIT, T, old0[:, SPLIT:T], gate0b)
         nc.sync.dma_start(out=out[0:P, :], in_=store[0][:])

@@ -44,16 +44,15 @@ def tile_picked_widxput_gate_l_kernel(tc, x_words, x_scales, mem, w1, slot, out)
         old0 = keep.tile([P, T], F32, name="old0")
         gate0a = keep.tile([P, SPLIT], F32, name="gate0a")
         gate1 = keep.tile([P, T], F32, name="gate1")
-        acc0a = psum.tile([P, SPLIT], F32, name="acc0a")
-        acc0b = psum.tile([P, T - SPLIT], F32, name="acc0b")
+        acc0 = [psum.tile([P, T], F32, name=f"acc0{g}") for g in range(2)]
         acc1 = psum.tile([P, T], F32, name="acc1")
 
         def w_rows(b, z):
             rows = w1[z * K_PASS : (z + 1) * K_PASS, b * P : (b + 1) * P]
             return rows.rearrange("(p j) m -> p j m", j=PACK)
 
-        def project(acc, lo, hi, codes, scales):
-            for z in range(PASSES):
+        def project(acc, lo, hi, codes, scales, passes=range(PASSES)):
+            for z in passes:
                 nc.tensor.matmul_mx(
                     out=acc,
                     lhsT=codes[z].bitcast(FP8X4),
@@ -69,14 +68,15 @@ def tile_picked_widxput_gate_l_kernel(tc, x_words, x_scales, mem, w1, slot, out)
 
         scale_rows = x_scales.rearrange("z (q r) c -> r q z c", r=4)
         nc.sync.dma_start(out=raw0[0][:], in_=w_rows(0, 0))
+        nc.sync.dma_start(out=raw0[1][:], in_=w_rows(0, 1))
         for r in range(4):
             nc.sync.dma_start(out=xs[r:P:32, :, :].bitcast(I32), in_=scale_rows[r].bitcast(I32))
-        nc.sync.dma_start(out=raw0[1][:], in_=w_rows(0, 1))
         x_cols = x_words.rearrange("z p c -> p z c")
         nc.sync.dma_start(out=xw[:, :, 0:2 * SPLIT].bitcast(I32), in_=x_cols[:, :, 0:2 * SPLIT].bitcast(I32))
         nc.sync.dma_start(out=store[0][:], in_=mem[0:P, :])
         nc.sync.dma_start(offsets[:], slot)
-        nc.sync.dma_start(out=xw[:, :, 2 * SPLIT:2 * T].bitcast(I32), in_=x_cols[:, :, 2 * SPLIT:2 * T].bitcast(I32))
+        for z in range(PASSES):
+            nc.sync.dma_start(out=xw[:, z, 2 * SPLIT : 2 * T].bitcast(I32), in_=x_cols[:, z, 2 * SPLIT : 2 * T].bitcast(I32))
         for z in range(PASSES):
             nc.sync.dma_start(
                 out=raw1[:, z * K_PASS : (z + 1) * K_PASS].rearrange("p (j m) -> p j m", j=PACK), in_=w_rows(1, z)
@@ -90,11 +90,15 @@ def tile_picked_widxput_gate_l_kernel(tc, x_words, x_scales, mem, w1, slot, out)
             )
         for z in range(PASSES):
             nc.vector.quantize_mx(out=codes0[z][:].bitcast(FP8X4), scales=scales0[z][:], in_=grouped0[z][:])
-        for lo in range(0, SPLIT, P):
-            project(acc0a[:, lo : lo + P], lo, lo + P, [t[:] for t in codes0], [t[:] for t in scales0])
+        w0 = ([t[:] for t in codes0], [t[:] for t in scales0])
+        for z in range(PASSES):
+            for g in range(2):
+                project(acc0[g][:, g * P : (g + 1) * P], g * P, (g + 1) * P, *w0, passes=[z])
+        for g in range(2):
+            cols = slice(g * P, (g + 1) * P)
+            nc.scalar.activation(out=gate0a[:, cols], in_=acc0[g][:, cols], func=SIGMOID)
         for lo in range(SPLIT, T, P):
-            project(acc0b[:, lo - SPLIT : lo - SPLIT + P], lo, lo + P, [t[:] for t in codes0], [t[:] for t in scales0])
-        nc.scalar.activation(out=gate0a[:], in_=acc0a[:], func=SIGMOID)
+            project(acc0[1][:, lo : lo + P], lo, lo + P, *w0)
         nc.vector.tensor_copy(old0[:], store[0][:].indirect(offsets[:]))
         scatter(0, 0, SPLIT, old0[:, 0:SPLIT], gate0a[:])
 
@@ -106,7 +110,7 @@ def tile_picked_widxput_gate_l_kernel(tc, x_words, x_scales, mem, w1, slot, out)
             )
         old1 = raw1[:, SPLIT : SPLIT + T]
         gate0b = raw1[:, SPLIT + T : 2 * T]
-        nc.scalar.activation(out=gate0b, in_=acc0b[:], func=SIGMOID)
+        nc.scalar.activation(out=gate0b, in_=acc0[1][:, SPLIT:T], func=SIGMOID)
         nc.vector.quantize_mx(out=codes1[:].bitcast(FP8X4), scales=scales1[:], in_=grouped1[:])
         project(
             acc1[:],

@@ -21,6 +21,8 @@ PACK = 4
 K_PASS = P * PACK
 PASSES = K // K_PASS
 SPLIT = 256
+EARLY = 256
+FIRST = 224
 
 
 def tile_picked_widxput_gate_l_kernel(tc, x_words, x_scales, mem, w1, slot, out):
@@ -33,7 +35,8 @@ def tile_picked_widxput_gate_l_kernel(tc, x_words, x_scales, mem, w1, slot, out)
         xw = keep.tile([P, PASSES, 2 * T], U8, name="xw", align_bytes=64)
         xs = keep.tile([P, PASSES, T], U8, name="xs", align_bytes=64)
         raw0 = [keep.tile([P, PACK, P], F32, name=f"raw0{z}") for z in range(PASSES)]
-        raw1 = keep.tile([P, PASSES * PACK * P], F32, name="raw1")
+        work = keep.tile([P, EARLY + PASSES * K_PASS], F32, name="work")
+        raw1 = [work[:, EARLY + (PASSES - 1 - z) * K_PASS : EARLY + (PASSES - z) * K_PASS] for z in range(PASSES)]
         grouped0 = [keep.tile([P, P * PACK], BF16, name=f"grouped0{z}", align_bytes=64) for z in range(PASSES)]
         grouped1 = keep.tile([P, PASSES * P * PACK], BF16, name="grouped1", align_bytes=64)
         codes0 = [keep.tile([P, P], U32, name=f"codes0{z}", align_bytes=64) for z in range(PASSES)]
@@ -42,7 +45,7 @@ def tile_picked_widxput_gate_l_kernel(tc, x_words, x_scales, mem, w1, slot, out)
         scales1 = keep.tile([P, PASSES * P], U8, name="scales1", align_bytes=64)
         store = [keep.tile([P, U], F32, name=f"store{b}") for b in range(2)]
         old0 = keep.tile([P, T], F32, name="old0")
-        gate0a = keep.tile([P, SPLIT], F32, name="gate0a")
+        gate0 = keep.tile([P, T], F32, name="gate0")
         gate1 = keep.tile([P, T], F32, name="gate1")
         acc0 = [psum.tile([P, T], F32, name=f"acc0{g}") for g in range(2)]
         acc1 = psum.tile([P, T], F32, name="acc1")
@@ -67,21 +70,21 @@ def tile_picked_widxput_gate_l_kernel(tc, x_words, x_scales, mem, w1, slot, out)
             nc.vector.tensor_tensor(store[b][:].indirect(offsets[:, lo // 16 : hi // 16]), old, gate, MULT)
 
         scale_rows = x_scales.rearrange("z (q r) c -> r q z c", r=4)
+        x_cols = x_words.rearrange("z p c -> p z c")
+        nc.sync.dma_start(offsets[:], slot)
         nc.sync.dma_start(out=raw0[0][:], in_=w_rows(0, 0))
         nc.sync.dma_start(out=raw0[1][:], in_=w_rows(0, 1))
         for r in range(4):
             nc.sync.dma_start(out=xs[r:P:32, :, :].bitcast(I32), in_=scale_rows[r].bitcast(I32))
-        x_cols = x_words.rearrange("z p c -> p z c")
-        nc.sync.dma_start(out=xw[:, :, 0:2 * SPLIT].bitcast(I32), in_=x_cols[:, :, 0:2 * SPLIT].bitcast(I32))
         nc.sync.dma_start(out=store[0][:], in_=mem[0:P, :])
-        nc.sync.dma_start(offsets[:], slot)
-        for z in range(PASSES):
-            nc.sync.dma_start(out=xw[:, z, 2 * SPLIT : 2 * T].bitcast(I32), in_=x_cols[:, z, 2 * SPLIT : 2 * T].bitcast(I32))
+        nc.sync.dma_start(out=xw[:, :, 0 : 2 * SPLIT].bitcast(I32), in_=x_cols[:, :, 0 : 2 * SPLIT].bitcast(I32))
+        nc.sync.dma_start(out=store[1][:], in_=mem[P : 2 * P, :])
         for z in range(PASSES):
             nc.sync.dma_start(
-                out=raw1[:, z * K_PASS : (z + 1) * K_PASS].rearrange("p (j m) -> p j m", j=PACK), in_=w_rows(1, z)
+                out=raw1[z].rearrange("p (j m) -> p j m", j=PACK), in_=w_rows(1, z)
             )
-        nc.sync.dma_start(out=store[1][:], in_=mem[P : 2 * P, :])
+        for z in reversed(range(PASSES)):
+            nc.sync.dma_start(out=xw[:, z, 2 * SPLIT : 2 * T].bitcast(I32), in_=x_cols[:, z, 2 * SPLIT : 2 * T].bitcast(I32))
 
         for z in range(PASSES):
             nc.vector.tensor_copy(
@@ -91,26 +94,24 @@ def tile_picked_widxput_gate_l_kernel(tc, x_words, x_scales, mem, w1, slot, out)
         for z in range(PASSES):
             nc.vector.quantize_mx(out=codes0[z][:].bitcast(FP8X4), scales=scales0[z][:], in_=grouped0[z][:])
         w0 = ([t[:] for t in codes0], [t[:] for t in scales0])
-        for z in range(PASSES):
-            for g in range(2):
-                project(acc0[g][:, g * P : (g + 1) * P], g * P, (g + 1) * P, *w0, passes=[z])
         for g in range(2):
             cols = slice(g * P, (g + 1) * P)
-            nc.scalar.activation(out=gate0a[:, cols], in_=acc0[g][:, cols], func=SIGMOID)
+            project(acc0[g][:, cols], g * P, (g + 1) * P, *w0)
+            nc.scalar.activation(out=gate0[:, cols], in_=acc0[g][:, cols], func=SIGMOID)
         for lo in range(SPLIT, T, P):
-            project(acc0[1][:, lo : lo + P], lo, lo + P, *w0)
+            project(acc0[0][:, lo : lo + P], lo, lo + P, *w0)
         nc.vector.tensor_copy(old0[:], store[0][:].indirect(offsets[:]))
-        scatter(0, 0, SPLIT, old0[:, 0:SPLIT], gate0a[:])
+        old1 = work[:, 0:T]
+        nc.vector.tensor_copy(work[:, 0:EARLY], store[1][:].indirect(offsets[:, 0 : EARLY // 16]))
+        scatter(0, 0, FIRST, old0[:, 0:FIRST], gate0[:, 0:FIRST])
 
         for z in range(PASSES):
             cols = slice(z * K_PASS, (z + 1) * K_PASS)
             nc.scalar.copy(
                 out=grouped1[:, cols].rearrange("p (c i j) -> p c j i", i=4, j=PACK),
-                in_=raw1[:, cols].rearrange("p (j c i) -> p c j i", j=PACK, i=4),
+                in_=raw1[z].rearrange("p (j c i) -> p c j i", j=PACK, i=4),
             )
-        old1 = raw1[:, SPLIT : SPLIT + T]
-        gate0b = raw1[:, SPLIT + T : 2 * T]
-        nc.scalar.activation(out=gate0b, in_=acc0[1][:, SPLIT:T], func=SIGMOID)
+        nc.scalar.activation(out=gate0[:, SPLIT:T], in_=acc0[0][:, SPLIT:T], func=SIGMOID)
         nc.vector.quantize_mx(out=codes1[:].bitcast(FP8X4), scales=scales1[:], in_=grouped1[:])
         project(
             acc1[:],
@@ -120,8 +121,8 @@ def tile_picked_widxput_gate_l_kernel(tc, x_words, x_scales, mem, w1, slot, out)
             [scales1[:, z * P : (z + 1) * P] for z in range(PASSES)],
         )
         nc.scalar.activation(out=gate1[:], in_=acc1[:], func=SIGMOID)
-        nc.vector.tensor_copy(old1, store[1][:].indirect(offsets[:]))
-        scatter(0, SPLIT, T, old0[:, SPLIT:T], gate0b)
+        nc.vector.tensor_copy(work[:, EARLY:T], store[1][:].indirect(offsets[:, EARLY // 16 : T // 16]))
+        scatter(0, FIRST, T, old0[:, FIRST:T], gate0[:, FIRST:T])
         nc.sync.dma_start(out=out[0:P, :], in_=store[0][:])
         scatter(1, 0, T, old1, gate1[:])
         nc.sync.dma_start(out=out[P : 2 * P, :], in_=store[1][:])

@@ -22,7 +22,7 @@ K_PASS = P * PACK
 PASSES = K // K_PASS
 SPLIT = 256
 EARLY = 256
-FIRST = 224
+FIRST = 256
 
 
 def tile_picked_widxput_gate_l_kernel(tc, x_words, x_scales, mem, w1, slot, out):
@@ -48,7 +48,7 @@ def tile_picked_widxput_gate_l_kernel(tc, x_words, x_scales, mem, w1, slot, out)
         gate0 = keep.tile([P, T], F32, name="gate0")
         gate1 = keep.tile([P, T], F32, name="gate1")
         acc0 = [psum.tile([P, T], F32, name=f"acc0{g}") for g in range(2)]
-        acc1 = psum.tile([P, T], F32, name="acc1")
+        acc1 = [psum.tile([P, T], F32, name=f"acc1{h}") for h in range(2)]
 
         def w_rows(b, z):
             rows = w1[z * K_PASS : (z + 1) * K_PASS, b * P : (b + 1) * P]
@@ -113,14 +113,15 @@ def tile_picked_widxput_gate_l_kernel(tc, x_words, x_scales, mem, w1, slot, out)
             )
         nc.scalar.activation(out=gate0[:, SPLIT:T], in_=acc0[0][:, SPLIT:T], func=SIGMOID)
         nc.vector.quantize_mx(out=codes1[:].bitcast(FP8X4), scales=scales1[:], in_=grouped1[:])
-        project(
-            acc1[:],
-            0,
-            T,
+        w1q = (
             [codes1[:, z * P : (z + 1) * P] for z in range(PASSES)],
             [scales1[:, z * P : (z + 1) * P] for z in range(PASSES)],
         )
-        nc.scalar.activation(out=gate1[:], in_=acc1[:], func=SIGMOID)
+        for h in range(2):
+            for lo in range(h * SPLIT, (h + 1) * SPLIT, P):
+                project(acc1[h][:, lo : lo + P], lo, lo + P, *w1q)
+            half = slice(h * SPLIT, (h + 1) * SPLIT)
+            nc.scalar.activation(out=gate1[:, half], in_=acc1[h][:, half], func=SIGMOID)
         nc.vector.tensor_copy(work[:, EARLY:T], store[1][:].indirect(offsets[:, EARLY // 16 : T // 16]))
         scatter(0, FIRST, T, old0[:, FIRST:T], gate0[:, FIRST:T])
         nc.sync.dma_start(out=out[0:P, :], in_=store[0][:])

@@ -48,7 +48,7 @@ def tile_picked_widxput_gate_l_kernel(tc, x_words, x_scales, mem, w1, slot, out)
         gate0 = keep.tile([P, T], F32, name="gate0")
         gate1 = keep.tile([P, T], F32, name="gate1")
         acc0 = [psum.tile([P, T], F32, name=f"acc0{g}") for g in range(2)]
-        acc1 = [psum.tile([P, T], F32, name=f"acc1{h}") for h in range(2)]
+        acc1 = psum.tile([P, T], F32, name="acc1")
 
         def w_rows(b, z):
             rows = w1[z * K_PASS : (z + 1) * K_PASS, b * P : (b + 1) * P]
@@ -98,8 +98,9 @@ def tile_picked_widxput_gate_l_kernel(tc, x_words, x_scales, mem, w1, slot, out)
             cols = slice(g * P, (g + 1) * P)
             project(acc0[g][:, cols], g * P, (g + 1) * P, *w0)
             nc.scalar.activation(out=gate0[:, cols], in_=acc0[g][:, cols], func=SIGMOID)
-        for lo in range(SPLIT, T, P):
-            project(acc0[0][:, lo : lo + P], lo, lo + P, *w0)
+        for g in range(2):
+            lo = SPLIT + g * P
+            project(acc0[g][:, lo : lo + P], lo, lo + P, *w0)
         nc.vector.tensor_copy(old0[:], store[0][:].indirect(offsets[:]))
         old1 = work[:, 0:T]
         nc.vector.tensor_copy(work[:, 0:EARLY], store[1][:].indirect(offsets[:, 0 : EARLY // 16]))
@@ -111,17 +112,23 @@ def tile_picked_widxput_gate_l_kernel(tc, x_words, x_scales, mem, w1, slot, out)
                 out=grouped1[:, cols].rearrange("p (c i j) -> p c j i", i=4, j=PACK),
                 in_=raw1[z].rearrange("p (j c i) -> p c j i", j=PACK, i=4),
             )
-        nc.scalar.activation(out=gate0[:, SPLIT:T], in_=acc0[0][:, SPLIT:T], func=SIGMOID)
-        nc.vector.quantize_mx(out=codes1[:].bitcast(FP8X4), scales=scales1[:], in_=grouped1[:])
+        for g in range(2):
+            cols = slice(SPLIT + g * P, SPLIT + (g + 1) * P)
+            nc.scalar.activation(out=gate0[:, cols], in_=acc0[g][:, cols], func=SIGMOID)
+        for z in range(PASSES):
+            nc.vector.quantize_mx(
+                out=codes1[:, z * P : (z + 1) * P].bitcast(FP8X4),
+                scales=scales1[:, z * P : (z + 1) * P],
+                in_=grouped1[:, z * K_PASS : (z + 1) * K_PASS],
+            )
         w1q = (
             [codes1[:, z * P : (z + 1) * P] for z in range(PASSES)],
             [scales1[:, z * P : (z + 1) * P] for z in range(PASSES)],
         )
-        for h in range(2):
-            for lo in range(h * SPLIT, (h + 1) * SPLIT, P):
-                project(acc1[h][:, lo : lo + P], lo, lo + P, *w1q)
-            half = slice(h * SPLIT, (h + 1) * SPLIT)
-            nc.scalar.activation(out=gate1[:, half], in_=acc1[h][:, half], func=SIGMOID)
+        for acc, first, last in [(acc1, SPLIT, T), (acc0[0], 0, P), (acc0[1], P, SPLIT)]:
+            for lo in range(first, last, P):
+                project(acc[:, lo : lo + P], lo, lo + P, *w1q)
+            nc.scalar.activation(out=gate1[:, first:last], in_=acc[:, first:last], func=SIGMOID)
         nc.vector.tensor_copy(work[:, EARLY:T], store[1][:].indirect(offsets[:, EARLY // 16 : T // 16]))
         scatter(0, FIRST, T, old0[:, FIRST:T], gate0[:, FIRST:T])
         nc.sync.dma_start(out=out[0:P, :], in_=store[0][:])

@@ -15,14 +15,13 @@ FP8X4 = mybir.dt.float8_e4m3fn_x4
 FP4X4 = mybir.dt.float4_e2m1fn_x4
 MULT = mybir.AluOpType.mult
 SIGMOID = mybir.ActivationFunctionType.Sigmoid
+COPY = mybir.ActivationFunctionType.Copy
 
 P = 128
 PACK = 4
 K_PASS = P * PACK
 PASSES = K // K_PASS
-SPLIT = 256
-EARLY = 256
-FIRST = 256
+HALF = T // 2
 
 
 def tile_picked_widxput_gate_l_kernel(tc, x_words, x_scales, mem, w1, slot, out):
@@ -34,103 +33,66 @@ def tile_picked_widxput_gate_l_kernel(tc, x_words, x_scales, mem, w1, slot, out)
         offsets = keep.tile([P, T // 16], U16, name="offsets")
         xw = keep.tile([P, PASSES, 2 * T], U8, name="xw", align_bytes=64)
         xs = keep.tile([P, PASSES, T], U8, name="xs", align_bytes=64)
-        raw0 = [keep.tile([P, PACK, P], F32, name=f"raw0{z}") for z in range(PASSES)]
-        work = keep.tile([P, EARLY + PASSES * K_PASS], F32, name="work")
-        raw1 = [work[:, EARLY + (PASSES - 1 - z) * K_PASS : EARLY + (PASSES - z) * K_PASS] for z in range(PASSES)]
-        grouped0 = [keep.tile([P, P * PACK], BF16, name=f"grouped0{z}", align_bytes=64) for z in range(PASSES)]
-        grouped1 = keep.tile([P, PASSES * P * PACK], BF16, name="grouped1", align_bytes=64)
-        codes0 = [keep.tile([P, P], U32, name=f"codes0{z}", align_bytes=64) for z in range(PASSES)]
-        scales0 = [keep.tile([P, P], U8, name=f"scales0{z}", align_bytes=64) for z in range(PASSES)]
-        codes1 = keep.tile([P, PASSES * P], U32, name="codes1", align_bytes=64)
-        scales1 = keep.tile([P, PASSES * P], U8, name="scales1", align_bytes=64)
+        raw = [[keep.tile([P, PACK, P], F32, name=f"raw{b}{z}") for z in range(PASSES)] for b in range(2)]
+        grouped = [[keep.tile([P, P * PACK], BF16, name=f"grouped{b}{z}", align_bytes=64) for z in range(PASSES)] for b in range(2)]
+        codes = [[keep.tile([P, P], U32, name=f"codes{b}{z}", align_bytes=64) for z in range(PASSES)] for b in range(2)]
+        scales = [[keep.tile([P, P], U8, name=f"scales{b}{z}", align_bytes=64) for z in range(PASSES)] for b in range(2)]
         store = [keep.tile([P, U], F32, name=f"store{b}") for b in range(2)]
-        old0 = keep.tile([P, T], F32, name="old0")
-        gate0 = keep.tile([P, T], F32, name="gate0")
-        gate1 = keep.tile([P, T], F32, name="gate1")
-        acc0 = [psum.tile([P, T], F32, name=f"acc0{g}") for g in range(2)]
-        acc1 = psum.tile([P, T], F32, name="acc1")
+        gate = [keep.tile([P, T], F32, name=f"gate{b}") for b in range(2)]
+        new0 = keep.tile([P, T], F32, name="new0")
+        old1 = keep.tile([P, T], F32, name="old1")
+        acc = [[psum.tile([P, T], F32, name=f"acc{b}{h}") for h in range(2)] for b in range(2)]
 
         def w_rows(b, z):
             rows = w1[z * K_PASS : (z + 1) * K_PASS, b * P : (b + 1) * P]
             return rows.rearrange("(p j) m -> p j m", j=PACK)
 
-        def project(acc, lo, hi, codes, scales, passes=range(PASSES)):
-            for z in passes:
-                nc.tensor.matmul_mx(
-                    out=acc,
-                    lhsT=codes[z].bitcast(FP8X4),
-                    lhsT_scale=scales[z],
-                    rhs=xw[:, z, 2 * lo : 2 * hi].bitcast(FP4X4),
-                    rhs_scale=xs[:, z, lo:hi],
-                    start=(z == 0),
-                    stop=(z == PASSES - 1),
-                )
+        def listed(b, h):
+            return store[b][:].indirect(offsets[:, h * HALF // 16 : (h + 1) * HALF // 16])
 
-        def scatter(b, lo, hi, old, gate):
-            nc.vector.tensor_tensor(store[b][:].indirect(offsets[:, lo // 16 : hi // 16]), old, gate, MULT)
+        def quantise(b):
+            for z in range(PASSES):
+                nc.vector.tensor_copy(
+                    out=grouped[b][z][:].rearrange("p (c i j) -> p c j i", i=4, j=PACK),
+                    in_=raw[b][z][:].rearrange("p j (c i) -> p c j i", i=4),
+                )
+            for z in range(PASSES):
+                nc.vector.quantize_mx(out=codes[b][z][:].bitcast(FP8X4), scales=scales[b][z][:], in_=grouped[b][z][:])
+
+        def gates(b):
+            for h in range(2):
+                lo, hi = h * HALF, (h + 1) * HALF
+                for z in range(PASSES):
+                    nc.tensor.matmul_mx(
+                        out=acc[b][h][:, 0:HALF],
+                        lhsT=codes[b][z][:].bitcast(FP8X4),
+                        lhsT_scale=scales[b][z][:],
+                        rhs=xw[:, z, 2 * lo : 2 * hi].bitcast(FP4X4),
+                        rhs_scale=xs[:, z, lo:hi],
+                        start=(z == 0),
+                        stop=(z == PASSES - 1),
+                    )
+                nc.scalar.activation(out=gate[b][:, lo:hi], in_=acc[b][h][:, 0:HALF], func=SIGMOID)
 
         scale_rows = x_scales.rearrange("z (q r) c -> r q z c", r=4)
-        x_cols = x_words.rearrange("z p c -> p z c")
         nc.sync.dma_start(offsets[:], slot)
-        nc.sync.dma_start(out=raw0[0][:], in_=w_rows(0, 0))
-        nc.sync.dma_start(out=raw0[1][:], in_=w_rows(0, 1))
+        for z in range(PASSES):
+            nc.sync.dma_start(out=raw[0][z][:], in_=w_rows(0, z))
         for r in range(4):
             nc.sync.dma_start(out=xs[r:P:32, :, :].bitcast(I32), in_=scale_rows[r].bitcast(I32))
-        nc.sync.dma_start(out=store[0][:], in_=mem[0:P, :])
-        nc.sync.dma_start(out=xw[:, :, 0 : 2 * SPLIT].bitcast(I32), in_=x_cols[:, :, 0 : 2 * SPLIT].bitcast(I32))
-        nc.sync.dma_start(out=store[1][:], in_=mem[P : 2 * P, :])
+        nc.sync.dma_start(out=xw[:].bitcast(I32), in_=x_words.rearrange("z p c -> p z c").bitcast(I32))
         for z in range(PASSES):
-            nc.sync.dma_start(
-                out=raw1[z].rearrange("p (j m) -> p j m", j=PACK), in_=w_rows(1, z)
-            )
-        for z in reversed(range(PASSES)):
-            nc.sync.dma_start(out=xw[:, z, 2 * SPLIT : 2 * T].bitcast(I32), in_=x_cols[:, z, 2 * SPLIT : 2 * T].bitcast(I32))
+            nc.sync.dma_start(out=raw[1][z][:], in_=w_rows(1, z))
+        for b in range(2):
+            nc.sync.dma_start(out=store[b][:], in_=mem[b * P : (b + 1) * P, :])
 
-        for z in range(PASSES):
-            nc.vector.tensor_copy(
-                out=grouped0[z][:].rearrange("p (c i j) -> p c j i", i=4, j=PACK),
-                in_=raw0[z][:].rearrange("p j (c i) -> p c j i", i=4),
-            )
-        for z in range(PASSES):
-            nc.vector.quantize_mx(out=codes0[z][:].bitcast(FP8X4), scales=scales0[z][:], in_=grouped0[z][:])
-        w0 = ([t[:] for t in codes0], [t[:] for t in scales0])
-        for g in range(2):
-            cols = slice(g * P, (g + 1) * P)
-            project(acc0[g][:, cols], g * P, (g + 1) * P, *w0)
-            nc.scalar.activation(out=gate0[:, cols], in_=acc0[g][:, cols], func=SIGMOID)
-        for g in range(2):
-            lo = SPLIT + g * P
-            project(acc0[g][:, lo : lo + P], lo, lo + P, *w0)
-        nc.vector.tensor_copy(old0[:], store[0][:].indirect(offsets[:]))
-        old1 = work[:, 0:T]
-        nc.vector.tensor_copy(work[:, 0:EARLY], store[1][:].indirect(offsets[:, 0 : EARLY // 16]))
-        scatter(0, 0, FIRST, old0[:, 0:FIRST], gate0[:, 0:FIRST])
-
-        for z in range(PASSES):
-            cols = slice(z * K_PASS, (z + 1) * K_PASS)
-            nc.scalar.copy(
-                out=grouped1[:, cols].rearrange("p (c i j) -> p c j i", i=4, j=PACK),
-                in_=raw1[z].rearrange("p (j c i) -> p c j i", j=PACK, i=4),
-            )
-        for g in range(2):
-            cols = slice(SPLIT + g * P, SPLIT + (g + 1) * P)
-            nc.scalar.activation(out=gate0[:, cols], in_=acc0[g][:, cols], func=SIGMOID)
-        for z in range(PASSES):
-            nc.vector.quantize_mx(
-                out=codes1[:, z * P : (z + 1) * P].bitcast(FP8X4),
-                scales=scales1[:, z * P : (z + 1) * P],
-                in_=grouped1[:, z * K_PASS : (z + 1) * K_PASS],
-            )
-        w1q = (
-            [codes1[:, z * P : (z + 1) * P] for z in range(PASSES)],
-            [scales1[:, z * P : (z + 1) * P] for z in range(PASSES)],
-        )
-        for acc, first, last in [(acc1, SPLIT, T), (acc0[0], 0, P), (acc0[1], P, SPLIT)]:
-            for lo in range(first, last, P):
-                project(acc[:, lo : lo + P], lo, lo + P, *w1q)
-            nc.scalar.activation(out=gate1[:, first:last], in_=acc[:, first:last], func=SIGMOID)
-        nc.vector.tensor_copy(work[:, EARLY:T], store[1][:].indirect(offsets[:, EARLY // 16 : T // 16]))
-        scatter(0, FIRST, T, old0[:, FIRST:T], gate0[:, FIRST:T])
+        for b in range(2):
+            quantise(b)
+            gates(b)
+        nc.vector.tensor_tensor(new0[:], store[0][:].indirect(offsets[:]), gate[0][:], MULT)
+        nc.vector.tensor_copy(old1[:], store[1][:].indirect(offsets[:]))
+        for h in range(2):
+            nc.scalar.activation(listed(0, h), new0[:, h * HALF : (h + 1) * HALF], COPY)
         nc.sync.dma_start(out=out[0:P, :], in_=store[0][:])
-        scatter(1, 0, T, old1, gate1[:])
+        nc.vector.tensor_tensor(store[1][:].indirect(offsets[:]), old1[:], gate[1][:], MULT)
         nc.sync.dma_start(out=out[P : 2 * P, :], in_=store[1][:])

@@ -22,6 +22,7 @@ PACK = 4
 K_PASS = P * PACK
 PASSES = K // K_PASS
 HALF = T // 2
+FUSED = 320
 
 
 def tile_picked_widxput_gate_l_kernel(tc, x_words, x_scales, mem, w1, slot, out):
@@ -40,15 +41,16 @@ def tile_picked_widxput_gate_l_kernel(tc, x_words, x_scales, mem, w1, slot, out)
         store = [keep.tile([P, U], F32, name=f"store{b}") for b in range(2)]
         gate = [keep.tile([P, T], F32, name=f"gate{b}") for b in range(2)]
         new0 = keep.tile([P, T], F32, name="new0")
+        old0 = keep.tile([P, T - FUSED], F32, name="old0")
         old1 = keep.tile([P, T], F32, name="old1")
-        acc = [[psum.tile([P, T], F32, name=f"acc{b}{h}") for h in range(2)] for b in range(2)]
+        banks = [psum.tile([P, T], F32, name=f"bank{i}") for i in range(3)]
 
         def w_rows(b, z):
             rows = w1[z * K_PASS : (z + 1) * K_PASS, b * P : (b + 1) * P]
             return rows.rearrange("(p j) m -> p j m", j=PACK)
 
-        def listed(b, h):
-            return store[b][:].indirect(offsets[:, h * HALF // 16 : (h + 1) * HALF // 16])
+        def listed(b, lo, hi):
+            return store[b][:].indirect(offsets[:, lo // 16 : hi // 16])
 
         def quantise(b):
             for z in range(PASSES):
@@ -59,20 +61,18 @@ def tile_picked_widxput_gate_l_kernel(tc, x_words, x_scales, mem, w1, slot, out)
             for z in range(PASSES):
                 nc.vector.quantize_mx(out=codes[b][z][:].bitcast(FP8X4), scales=scales[b][z][:], in_=grouped[b][z][:])
 
-        def gates(b):
-            for h in range(2):
-                lo, hi = h * HALF, (h + 1) * HALF
-                for z in range(PASSES):
-                    nc.tensor.matmul_mx(
-                        out=acc[b][h][:, 0:HALF],
-                        lhsT=codes[b][z][:].bitcast(FP8X4),
-                        lhsT_scale=scales[b][z][:],
-                        rhs=xw[:, z, 2 * lo : 2 * hi].bitcast(FP4X4),
-                        rhs_scale=xs[:, z, lo:hi],
-                        start=(z == 0),
-                        stop=(z == PASSES - 1),
-                    )
-                nc.scalar.activation(out=gate[b][:, lo:hi], in_=acc[b][h][:, 0:HALF], func=SIGMOID)
+        def gates(b, lo, hi, bank):
+            for z in range(PASSES):
+                nc.tensor.matmul_mx(
+                    out=bank[:, lo:hi],
+                    lhsT=codes[b][z][:].bitcast(FP8X4),
+                    lhsT_scale=scales[b][z][:],
+                    rhs=xw[:, z, 2 * lo : 2 * hi].bitcast(FP4X4),
+                    rhs_scale=xs[:, z, lo:hi],
+                    start=(z == 0),
+                    stop=(z == PASSES - 1),
+                )
+            nc.scalar.activation(out=gate[b][:, lo:hi], in_=bank[:, lo:hi], func=SIGMOID)
 
         scale_rows = x_scales.rearrange("z (q r) c -> r q z c", r=4)
         nc.sync.dma_start(offsets[:], slot)
@@ -86,13 +86,17 @@ def tile_picked_widxput_gate_l_kernel(tc, x_words, x_scales, mem, w1, slot, out)
         for b in range(2):
             nc.sync.dma_start(out=store[b][:], in_=mem[b * P : (b + 1) * P, :])
 
-        for b in range(2):
-            quantise(b)
-            gates(b)
-        nc.vector.tensor_tensor(new0[:], store[0][:].indirect(offsets[:]), gate[0][:], MULT)
-        nc.vector.tensor_copy(old1[:], store[1][:].indirect(offsets[:]))
-        for h in range(2):
-            nc.scalar.activation(listed(0, h), new0[:, h * HALF : (h + 1) * HALF], COPY)
-        nc.sync.dma_start(out=out[0:P, :], in_=store[0][:])
-        nc.vector.tensor_tensor(store[1][:].indirect(offsets[:]), old1[:], gate[1][:], MULT)
+        quantise(0)
+        gates(0, 0, HALF, banks[0])
+        gates(0, HALF, T, banks[1])
+        quantise(1)
+        nc.vector.tensor_tensor(new0[:, 0:FUSED], listed(0, 0, FUSED), gate[0][:, 0:FUSED], MULT)
+        nc.scalar.activation(old0[:], listed(0, FUSED, T), COPY)
+        gates(1, 0, T, banks[2])
+        nc.vector.tensor_copy(old1[:], listed(1, 0, T))
+        nc.vector.tensor_tensor(new0[:, FUSED:T], old0[:], gate[0][:, FUSED:T], MULT)
+        for lo, hi in [(0, FUSED), (FUSED, T)]:
+            nc.scalar.activation(listed(0, lo, hi), new0[:, lo:hi], COPY)
+        nc.scalar.dma_start(out=out[0:P, :], in_=store[0][:])
+        nc.vector.tensor_tensor(listed(1, 0, T), old1[:], gate[1][:], MULT)
         nc.sync.dma_start(out=out[P : 2 * P, :], in_=store[1][:])

@@ -22,7 +22,8 @@ PACK = 4
 K_PASS = P * PACK
 PASSES = K // K_PASS
 HALF = T // 2
-FUSED = 320
+FUSED = 160
+FIRST = 128
 
 
 def tile_picked_widxput_gate_l_kernel(tc, x_words, x_scales, mem, w1, slot, out):
@@ -35,15 +36,16 @@ def tile_picked_widxput_gate_l_kernel(tc, x_words, x_scales, mem, w1, slot, out)
         xw = keep.tile([P, PASSES, 2 * T], U8, name="xw", align_bytes=64)
         xs = keep.tile([P, PASSES, T], U8, name="xs", align_bytes=64)
         raw = [[keep.tile([P, PACK, P], F32, name=f"raw{b}{z}") for z in range(PASSES)] for b in range(2)]
-        grouped = [[keep.tile([P, P * PACK], BF16, name=f"grouped{b}{z}", align_bytes=64) for z in range(PASSES)] for b in range(2)]
+        new0 = keep.tile([P, T], F32, name="new0", align_bytes=64)
+        woven = [keep.tile([P, K_PASS], BF16, name=f"woven{i}", align_bytes=64) for i in range(3)]
+        grouped = [[woven[0][:], woven[1][:]], [woven[2][:], new0[:, HALF:T].bitcast(BF16)]]
         codes = [[keep.tile([P, P], U32, name=f"codes{b}{z}", align_bytes=64) for z in range(PASSES)] for b in range(2)]
         scales = [[keep.tile([P, P], U8, name=f"scales{b}{z}", align_bytes=64) for z in range(PASSES)] for b in range(2)]
         store = [keep.tile([P, U], F32, name=f"store{b}") for b in range(2)]
         gate = [keep.tile([P, T], F32, name=f"gate{b}") for b in range(2)]
-        new0 = keep.tile([P, T], F32, name="new0")
         old0 = keep.tile([P, T - FUSED], F32, name="old0")
         old1 = keep.tile([P, T], F32, name="old1")
-        banks = [psum.tile([P, T], F32, name=f"bank{i}") for i in range(3)]
+        banks = [psum.tile([P, T], F32, name=f"bank{i}") for i in range(5)]
 
         def w_rows(b, z):
             rows = w1[z * K_PASS : (z + 1) * K_PASS, b * P : (b + 1) * P]
@@ -52,14 +54,14 @@ def tile_picked_widxput_gate_l_kernel(tc, x_words, x_scales, mem, w1, slot, out)
         def listed(b, lo, hi):
             return store[b][:].indirect(offsets[:, lo // 16 : hi // 16])
 
-        def quantise(b):
-            for z in range(PASSES):
+        def quantise(b, passes):
+            for z in passes:
                 nc.vector.tensor_copy(
-                    out=grouped[b][z][:].rearrange("p (c i j) -> p c j i", i=4, j=PACK),
+                    out=grouped[b][z].rearrange("p (c i j) -> p c j i", i=4, j=PACK),
                     in_=raw[b][z][:].rearrange("p j (c i) -> p c j i", i=4),
                 )
-            for z in range(PASSES):
-                nc.vector.quantize_mx(out=codes[b][z][:].bitcast(FP8X4), scales=scales[b][z][:], in_=grouped[b][z][:])
+            for z in passes:
+                nc.vector.quantize_mx(out=codes[b][z][:].bitcast(FP8X4), scales=scales[b][z][:], in_=grouped[b][z])
 
         def gates(b, lo, hi, bank):
             for z in range(PASSES):
@@ -75,28 +77,31 @@ def tile_picked_widxput_gate_l_kernel(tc, x_words, x_scales, mem, w1, slot, out)
             nc.scalar.activation(out=gate[b][:, lo:hi], in_=bank[:, lo:hi], func=SIGMOID)
 
         scale_rows = x_scales.rearrange("z (q r) c -> r q z c", r=4)
-        nc.sync.dma_start(offsets[:], slot)
         for z in range(PASSES):
             nc.sync.dma_start(out=raw[0][z][:], in_=w_rows(0, z))
-        for r in range(4):
-            nc.sync.dma_start(out=xs[r:P:32, :, :].bitcast(I32), in_=scale_rows[r].bitcast(I32))
+            for r in (2 * z, 2 * z + 1):
+                nc.sync.dma_start(out=xs[r:P:32, :, :].bitcast(I32), in_=scale_rows[r].bitcast(I32))
         nc.sync.dma_start(out=xw[:].bitcast(I32), in_=x_words.rearrange("z p c -> p z c").bitcast(I32))
-        for z in range(PASSES):
-            nc.sync.dma_start(out=raw[1][z][:], in_=w_rows(1, z))
-        for b in range(2):
-            nc.sync.dma_start(out=store[b][:], in_=mem[b * P : (b + 1) * P, :])
+        nc.sync.dma_start(out=raw[1][0][:], in_=w_rows(1, 0))
+        nc.sync.dma_start(offsets[:], slot)
+        nc.sync.dma_start(out=store[0][:], in_=mem[0:P, :])
+        nc.sync.dma_start(out=raw[1][1][:], in_=w_rows(1, 1))
+        nc.sync.dma_start(out=store[1][:], in_=mem[P : 2 * P, :])
 
-        quantise(0)
+        quantise(0, range(PASSES))
         gates(0, 0, HALF, banks[0])
         gates(0, HALF, T, banks[1])
-        quantise(1)
+        quantise(1, [0])
         nc.vector.tensor_tensor(new0[:, 0:FUSED], listed(0, 0, FUSED), gate[0][:, 0:FUSED], MULT)
         nc.scalar.activation(old0[:], listed(0, FUSED, T), COPY)
-        gates(1, 0, T, banks[2])
+        nc.scalar.activation(listed(0, 0, FIRST), new0[:, 0:FIRST], COPY)
+        quantise(1, [1])
+        gates(1, 0, HALF, banks[2])
+        gates(1, HALF, HALF + P, banks[3])
+        gates(1, HALF + P, T, banks[4])
         nc.vector.tensor_copy(old1[:], listed(1, 0, T))
-        nc.vector.tensor_tensor(new0[:, FUSED:T], old0[:], gate[0][:, FUSED:T], MULT)
-        for lo, hi in [(0, FUSED), (FUSED, T)]:
-            nc.scalar.activation(listed(0, lo, hi), new0[:, lo:hi], COPY)
+        nc.gpsimd.tensor_tensor(new0[:, FUSED:T], old0[:], gate[0][:, FUSED:T], MULT)
+        nc.scalar.activation(listed(0, FIRST, T), new0[:, FIRST:T], COPY)
         nc.scalar.dma_start(out=out[0:P, :], in_=store[0][:])
         nc.vector.tensor_tensor(listed(1, 0, T), old1[:], gate[1][:], MULT)
         nc.sync.dma_start(out=out[P : 2 * P, :], in_=store[1][:])

@@ -23,7 +23,7 @@ K_PASS = P * PACK
 PASSES = K // K_PASS
 HALF = T // 2
 FUSED = 160
-FIRST = 128
+FIRST = 160
 
 
 def tile_picked_widxput_gate_l_kernel(tc, x_words, x_scales, mem, w1, slot, out):

@@ -22,8 +22,9 @@ PACK = 4
 K_PASS = P * PACK
 PASSES = K // K_PASS
 HALF = T // 2
+FIRST = 128
 FUSED = 160
-FIRST = 160
+SHARE = 64
 
 
 def tile_picked_widxput_gate_l_kernel(tc, x_words, x_scales, mem, w1, slot, out):
@@ -35,15 +36,17 @@ def tile_picked_widxput_gate_l_kernel(tc, x_words, x_scales, mem, w1, slot, out)
         offsets = keep.tile([P, T // 16], U16, name="offsets")
         xw = keep.tile([P, PASSES, 2 * T], U8, name="xw", align_bytes=64)
         xs = keep.tile([P, PASSES, T], U8, name="xs", align_bytes=64)
-        raw = [[keep.tile([P, PACK, P], F32, name=f"raw{b}{z}") for z in range(PASSES)] for b in range(2)]
-        new0 = keep.tile([P, T], F32, name="new0", align_bytes=64)
+        staged = [keep.tile([P, PACK, P], F32, name=f"raw{i}") for i in range(3)]
+        pitch = P + HALF
+        late = keep.tile([P, FUSED + PACK * pitch], F32, name="late", align_bytes=64)
+        raw = [[staged[0], staged[1]], [staged[2], late[:, FUSED:].rearrange("p (j m) -> p j m", j=PACK)[:, :, 0:P]]]
         woven = [keep.tile([P, K_PASS], BF16, name=f"woven{i}", align_bytes=64) for i in range(3)]
-        grouped = [[woven[0][:], woven[1][:]], [woven[2][:], new0[:, HALF:T].bitcast(BF16)]]
+        grouped = [[woven[0][:], woven[1][:]], [woven[2][:], late[:, FUSED + P : FUSED + pitch].bitcast(BF16)]]
         codes = [[keep.tile([P, P], U32, name=f"codes{b}{z}", align_bytes=64) for z in range(PASSES)] for b in range(2)]
         scales = [[keep.tile([P, P], U8, name=f"scales{b}{z}", align_bytes=64) for z in range(PASSES)] for b in range(2)]
         store = [keep.tile([P, U], F32, name=f"store{b}") for b in range(2)]
         gate = [keep.tile([P, T], F32, name=f"gate{b}") for b in range(2)]
-        old0 = keep.tile([P, T - FUSED], F32, name="old0")
+        old0 = keep.tile([P, T], F32, name="old0")
         old1 = keep.tile([P, T], F32, name="old1")
         banks = [psum.tile([P, T], F32, name=f"bank{i}") for i in range(5)]
 
@@ -92,16 +95,19 @@ def tile_picked_widxput_gate_l_kernel(tc, x_words, x_scales, mem, w1, slot, out)
         gates(0, 0, HALF, banks[0])
         gates(0, HALF, T, banks[1])
         quantise(1, [0])
-        nc.vector.tensor_tensor(new0[:, 0:FUSED], listed(0, 0, FUSED), gate[0][:, 0:FUSED], MULT)
-        nc.scalar.activation(old0[:], listed(0, FUSED, T), COPY)
-        nc.scalar.activation(listed(0, 0, FIRST), new0[:, 0:FIRST], COPY)
+        nc.vector.tensor_tensor(late[:, 0:FUSED], listed(0, 0, FUSED), gate[0][:, 0:FUSED], MULT)
+        nc.scalar.activation(old0[:, FUSED:T], listed(0, FUSED, T), COPY)
+        nc.scalar.activation(listed(0, 0, FIRST), late[:, 0:FIRST], COPY)
         quantise(1, [1])
+        mid = FUSED + P
+        nc.vector.tensor_tensor(late[:, FUSED:mid], old0[:, FUSED:mid], gate[0][:, FUSED:mid], MULT)
+        nc.scalar.activation(old1[:, T - SHARE : T], listed(1, T - SHARE, T), COPY)
         gates(1, 0, HALF, banks[2])
         gates(1, HALF, HALF + P, banks[3])
         gates(1, HALF + P, T, banks[4])
-        nc.vector.tensor_copy(old1[:], listed(1, 0, T))
-        nc.gpsimd.tensor_tensor(new0[:, FUSED:T], old0[:], gate[0][:, FUSED:T], MULT)
-        nc.scalar.activation(listed(0, FIRST, T), new0[:, FIRST:T], COPY)
-        nc.scalar.dma_start(out=out[0:P, :], in_=store[0][:])
+        nc.vector.tensor_copy(old1[:, 0 : T - SHARE], listed(1, 0, T - SHARE))
+        nc.gpsimd.tensor_tensor(late[:, mid:T], old0[:, mid:T], gate[0][:, mid:T], MULT)
+        nc.scalar.activation(listed(0, FIRST, T), late[:, FIRST:T], COPY)
+        nc.sync.dma_start(out=out[0:P, :], in_=store[0][:])
         nc.vector.tensor_tensor(listed(1, 0, T), old1[:], gate[1][:], MULT)
         nc.sync.dma_start(out=out[P : 2 * P, :], in_=store[1][:])

@@ -23,7 +23,7 @@ K_PASS = P * PACK
 PASSES = K // K_PASS
 HALF = T // 2
 FIRST = 128
-FUSED = 160
+FUSED = 224
 SHARE = 64
 
 

@@ -48,7 +48,7 @@ def tile_picked_widxput_gate_l_kernel(tc, x_words, x_scales, mem, w1, slot, out)
         gate = [keep.tile([P, T], F32, name=f"gate{b}") for b in range(2)]
         old0 = keep.tile([P, T], F32, name="old0")
         old1 = keep.tile([P, T], F32, name="old1")
-        banks = [psum.tile([P, T], F32, name=f"bank{i}") for i in range(5)]
+        banks = [psum.tile([P, T], F32, name=f"bank{i}") for i in range(6)]
 
         def w_rows(b, z):
             rows = w1[z * K_PASS : (z + 1) * K_PASS, b * P : (b + 1) * P]
@@ -102,9 +102,8 @@ def tile_picked_widxput_gate_l_kernel(tc, x_words, x_scales, mem, w1, slot, out)
         mid = FUSED + P
         nc.vector.tensor_tensor(late[:, FUSED:mid], old0[:, FUSED:mid], gate[0][:, FUSED:mid], MULT)
         nc.scalar.activation(old1[:, T - SHARE : T], listed(1, T - SHARE, T), COPY)
-        gates(1, 0, HALF, banks[2])
-        gates(1, HALF, HALF + P, banks[3])
-        gates(1, HALF + P, T, banks[4])
+        for g in range(T // P):
+            gates(1, g * P, (g + 1) * P, banks[2 + g])
         nc.vector.tensor_copy(old1[:, 0 : T - SHARE], listed(1, 0, T - SHARE))
         nc.gpsimd.tensor_tensor(late[:, mid:T], old0[:, mid:T], gate[0][:, mid:T], MULT)
         nc.scalar.activation(listed(0, FIRST, T), late[:, FIRST:T], COPY)

@@ -36,12 +36,10 @@ def tile_picked_widxput_gate_l_kernel(tc, x_words, x_scales, mem, w1, slot, out)
         offsets = keep.tile([P, T // 16], U16, name="offsets")
         xw = keep.tile([P, PASSES, 2 * T], U8, name="xw", align_bytes=64)
         xs = keep.tile([P, PASSES, T], U8, name="xs", align_bytes=64)
-        staged = [keep.tile([P, PACK, P], F32, name=f"raw{i}") for i in range(3)]
-        pitch = P + HALF
-        late = keep.tile([P, FUSED + PACK * pitch], F32, name="late", align_bytes=64)
-        raw = [[staged[0], staged[1]], [staged[2], late[:, FUSED:].rearrange("p (j m) -> p j m", j=PACK)[:, :, 0:P]]]
+        raw = [[keep.tile([P, PACK, P], F32, name=f"raw{b}{z}") for z in range(PASSES)] for b in range(2)]
+        late = keep.tile([P, T], F32, name="late", align_bytes=64)
         woven = [keep.tile([P, K_PASS], BF16, name=f"woven{i}", align_bytes=64) for i in range(3)]
-        grouped = [[woven[0][:], woven[1][:]], [woven[2][:], late[:, FUSED + P : FUSED + pitch].bitcast(BF16)]]
+        grouped = [[woven[0][:], woven[1][:]], [woven[2][:], late[:, FUSED : FUSED + HALF].bitcast(BF16)]]
         codes = [[keep.tile([P, P], U32, name=f"codes{b}{z}", align_bytes=64) for z in range(PASSES)] for b in range(2)]
         scales = [[keep.tile([P, P], U8, name=f"scales{b}{z}", align_bytes=64) for z in range(PASSES)] for b in range(2)]
         store = [keep.tile([P, U], F32, name=f"store{b}") for b in range(2)]
@@ -57,14 +55,18 @@ def tile_picked_widxput_gate_l_kernel(tc, x_words, x_scales, mem, w1, slot, out)
         def listed(b, lo, hi):
             return store[b][:].indirect(offsets[:, lo // 16 : hi // 16])
 
-        def quantise(b, passes):
-            for z in passes:
+        def quantise(b, pieces):
+            for z, lo, hi in pieces:
                 nc.vector.tensor_copy(
-                    out=grouped[b][z].rearrange("p (c i j) -> p c j i", i=4, j=PACK),
-                    in_=raw[b][z][:].rearrange("p j (c i) -> p c j i", i=4),
+                    out=grouped[b][z][:, PACK * lo : PACK * hi].rearrange("p (c i j) -> p c j i", i=4, j=PACK),
+                    in_=raw[b][z][:, :, lo:hi].rearrange("p j (c i) -> p c j i", i=4),
                 )
-            for z in passes:
-                nc.vector.quantize_mx(out=codes[b][z][:].bitcast(FP8X4), scales=scales[b][z][:], in_=grouped[b][z])
+            for z, lo, hi in pieces:
+                nc.vector.quantize_mx(
+                    out=codes[b][z][:, lo:hi].bitcast(FP8X4),
+                    scales=scales[b][z][:, lo:hi],
+                    in_=grouped[b][z][:, PACK * lo : PACK * hi],
+                )
 
         def gates(b, lo, hi, bank):
             for z in range(PASSES):
@@ -91,14 +93,14 @@ def tile_picked_widxput_gate_l_kernel(tc, x_words, x_scales, mem, w1, slot, out)
         nc.sync.dma_start(out=raw[1][1][:], in_=w_rows(1, 1))
         nc.sync.dma_start(out=store[1][:], in_=mem[P : 2 * P, :])
 
-        quantise(0, range(PASSES))
+        quantise(0, [(0, 0, P), (1, 0, P)])
         gates(0, 0, HALF, banks[0])
         gates(0, HALF, T, banks[1])
-        quantise(1, [0])
+        quantise(1, [(0, 0, P)])
         nc.vector.tensor_tensor(late[:, 0:FUSED], listed(0, 0, FUSED), gate[0][:, 0:FUSED], MULT)
         nc.scalar.activation(old0[:, FUSED:T], listed(0, FUSED, T), COPY)
         nc.scalar.activation(listed(0, 0, FIRST), late[:, 0:FIRST], COPY)
-        quantise(1, [1])
+        quantise(1, [(1, 0, P // 2), (1, P // 2, P)])
         mid = FUSED + P
         nc.vector.tensor_tensor(late[:, FUSED:mid], old0[:, FUSED:mid], gate[0][:, FUSED:mid], MULT)
         nc.scalar.activation(old1[:, T - SHARE : T], listed(1, T - SHARE, T), COPY)

@@ -46,7 +46,7 @@ def tile_picked_widxput_gate_l_kernel(tc, x_words, x_scales, mem, w1, slot, out)
         gate = [keep.tile([P, T], F32, name=f"gate{b}") for b in range(2)]
         old0 = keep.tile([P, T], F32, name="old0")
         old1 = keep.tile([P, T], F32, name="old1")
-        banks = [psum.tile([P, T], F32, name=f"bank{i}") for i in range(6)]
+        banks = [psum.tile([P, T], F32, name=f"bank{i}") for i in range(8)]
 
         def w_rows(b, z):
             rows = w1[z * K_PASS : (z + 1) * K_PASS, b * P : (b + 1) * P]
@@ -93,9 +93,10 @@ def tile_picked_widxput_gate_l_kernel(tc, x_words, x_scales, mem, w1, slot, out)
         nc.sync.dma_start(out=raw[1][1][:], in_=w_rows(1, 1))
         nc.sync.dma_start(out=store[1][:], in_=mem[P : 2 * P, :])
 
-        quantise(0, [(0, 0, P), (1, 0, P)])
-        gates(0, 0, HALF, banks[0])
-        gates(0, HALF, T, banks[1])
+        quantise(0, [(0, 0, P)])
+        quantise(0, [(1, 0, P // 2), (1, P // 2, P)])
+        for g in range(T // P):
+            gates(0, g * P, (g + 1) * P, banks[g])
         quantise(1, [(0, 0, P)])
         nc.vector.tensor_tensor(late[:, 0:FUSED], listed(0, 0, FUSED), gate[0][:, 0:FUSED], MULT)
         nc.scalar.activation(old0[:, FUSED:T], listed(0, FUSED, T), COPY)
@@ -105,7 +106,7 @@ def tile_picked_widxput_gate_l_kernel(tc, x_words, x_scales, mem, w1, slot, out)
         nc.vector.tensor_tensor(late[:, FUSED:mid], old0[:, FUSED:mid], gate[0][:, FUSED:mid], MULT)
         nc.scalar.activation(old1[:, T - SHARE : T], listed(1, T - SHARE, T), COPY)
         for g in range(T // P):
-            gates(1, g * P, (g + 1) * P, banks[2 + g])
+            gates(1, g * P, (g + 1) * P, banks[4 + g])
         nc.vector.tensor_copy(old1[:, 0 : T - SHARE], listed(1, 0, T - SHARE))
         nc.gpsimd.tensor_tensor(late[:, mid:T], old0[:, mid:T], gate[0][:, mid:T], MULT)
         nc.scalar.activation(listed(0, FIRST, T), late[:, FIRST:T], COPY)

@@ -25,6 +25,7 @@ HALF = T // 2
 FIRST = 128
 FUSED = 224
 SHARE = 64
+AXI = 256
 
 
 def tile_picked_widxput_gate_l_kernel(tc, x_words, x_scales, mem, w1, slot, out):
@@ -33,16 +34,16 @@ def tile_picked_widxput_gate_l_kernel(tc, x_words, x_scales, mem, w1, slot, out)
         keep = ctx.enter_context(tc.tile_pool(name="keep", bufs=1))
         psum = ctx.enter_context(tc.psum_pool(name="psum", bufs=1))
 
-        offsets = keep.tile([P, T // 16], U16, name="offsets")
-        xw = keep.tile([P, PASSES, 2 * T], U8, name="xw", align_bytes=64)
-        xs = keep.tile([P, PASSES, T], U8, name="xs", align_bytes=64)
-        raw = [[keep.tile([P, PACK, P], F32, name=f"raw{b}{z}") for z in range(PASSES)] for b in range(2)]
+        offsets = keep.tile([P, T // 16], U16, name="offsets", align_bytes=AXI)
+        xw = keep.tile([P, PASSES, 2 * T], U8, name="xw", align_bytes=AXI)
+        xs = keep.tile([P, PASSES, T], U8, name="xs", align_bytes=AXI)
+        raw = [[keep.tile([P, PACK, P], F32, name=f"raw{b}{z}", align_bytes=AXI) for z in range(PASSES)] for b in range(2)]
         late = keep.tile([P, T], F32, name="late", align_bytes=64)
         woven = [keep.tile([P, K_PASS], BF16, name=f"woven{i}", align_bytes=64) for i in range(3)]
         grouped = [[woven[0][:], woven[1][:]], [woven[2][:], late[:, FUSED : FUSED + HALF].bitcast(BF16)]]
         codes = [[keep.tile([P, P], U32, name=f"codes{b}{z}", align_bytes=64) for z in range(PASSES)] for b in range(2)]
         scales = [[keep.tile([P, P], U8, name=f"scales{b}{z}", align_bytes=64) for z in range(PASSES)] for b in range(2)]
-        store = [keep.tile([P, U], F32, name=f"store{b}") for b in range(2)]
+        store = [keep.tile([P, U], F32, name=f"store{b}", align_bytes=AXI) for b in range(2)]
         gate = [keep.tile([P, T], F32, name=f"gate{b}") for b in range(2)]
         old0 = keep.tile([P, T], F32, name="old0")
         old1 = keep.tile([P, T], F32, name="old1")

@@ -24,7 +24,6 @@ PASSES = K // K_PASS
 HALF = T // 2
 FIRST = 128
 FUSED = 224
-SHARE = 64
 AXI = 256
 
 
@@ -105,10 +104,9 @@ def tile_picked_widxput_gate_l_kernel(tc, x_words, x_scales, mem, w1, slot, out)
         quantise(1, [(1, 0, P // 2), (1, P // 2, P)])
         mid = FUSED + P
         nc.vector.tensor_tensor(late[:, FUSED:mid], old0[:, FUSED:mid], gate[0][:, FUSED:mid], MULT)
-        nc.scalar.activation(old1[:, T - SHARE : T], listed(1, T - SHARE, T), COPY)
         for g in range(T // P):
             gates(1, g * P, (g + 1) * P, banks[4 + g])
-        nc.vector.tensor_copy(old1[:, 0 : T - SHARE], listed(1, 0, T - SHARE))
+        nc.vector.tensor_copy(old1[:], listed(1, 0, T))
         nc.gpsimd.tensor_tensor(late[:, mid:T], old0[:, mid:T], gate[0][:, mid:T], MULT)
         nc.scalar.activation(listed(0, FIRST, T), late[:, FIRST:T], COPY)
         nc.sync.dma_start(out=out[0:P, :], in_=store[0][:])

@@ -23,7 +23,7 @@ K_PASS = P * PACK
 PASSES = K // K_PASS
 HALF = T // 2
 FIRST = 128
-FUSED = 224
+FUSED = 192
 AXI = 256
 
 
@@ -102,12 +102,10 @@ def tile_picked_widxput_gate_l_kernel(tc, x_words, x_scales, mem, w1, slot, out)
         nc.scalar.activation(old0[:, FUSED:T], listed(0, FUSED, T), COPY)
         nc.scalar.activation(listed(0, 0, FIRST), late[:, 0:FIRST], COPY)
         quantise(1, [(1, 0, P // 2), (1, P // 2, P)])
-        mid = FUSED + P
-        nc.vector.tensor_tensor(late[:, FUSED:mid], old0[:, FUSED:mid], gate[0][:, FUSED:mid], MULT)
         for g in range(T // P):
             gates(1, g * P, (g + 1) * P, banks[4 + g])
         nc.vector.tensor_copy(old1[:], listed(1, 0, T))
-        nc.gpsimd.tensor_tensor(late[:, mid:T], old0[:, mid:T], gate[0][:, mid:T], MULT)
+        nc.gpsimd.tensor_tensor(late[:, FUSED:T], old0[:, FUSED:T], gate[0][:, FUSED:T], MULT)
         nc.scalar.activation(listed(0, FIRST, T), late[:, FIRST:T], COPY)
         nc.sync.dma_start(out=out[0:P, :], in_=store[0][:])
         nc.vector.tensor_tensor(listed(1, 0, T), old1[:], gate[1][:], MULT)

@@ -36,7 +36,9 @@ def tile_picked_widxput_gate_l_kernel(tc, x_words, x_scales, mem, w1, slot, out)
         offsets = keep.tile([P, T // 16], U16, name="offsets", align_bytes=AXI)
         xw = keep.tile([P, PASSES, 2 * T], U8, name="xw", align_bytes=AXI)
         xs = keep.tile([P, PASSES, T], U8, name="xs", align_bytes=AXI)
-        raw = [[keep.tile([P, PACK, P], F32, name=f"raw{b}{z}", align_bytes=AXI) for z in range(PASSES)] for b in range(2)]
+        raw = [[keep.tile([P, PACK, P], F32, name=f"raw{b}{z}", align_bytes=AXI) for z in range(PASSES - b)] for b in range(2)]
+        wide = keep.tile([P, PACK, N], F32, name="wide", align_bytes=AXI)
+        rows_of = [[raw[0][0][:], raw[0][1][:]], [raw[1][0][:], wide[:, :, 0:P]]]
         late = keep.tile([P, T], F32, name="late", align_bytes=64)
         woven = [keep.tile([P, K_PASS], BF16, name=f"woven{i}", align_bytes=64) for i in range(3)]
         grouped = [[woven[0][:], woven[1][:]], [woven[2][:], late[:, FUSED : FUSED + HALF].bitcast(BF16)]]
@@ -59,7 +61,7 @@ def tile_picked_widxput_gate_l_kernel(tc, x_words, x_scales, mem, w1, slot, out)
             for z, lo, hi in pieces:
                 nc.vector.tensor_copy(
                     out=grouped[b][z][:, PACK * lo : PACK * hi].rearrange("p (c i j) -> p c j i", i=4, j=PACK),
-                    in_=raw[b][z][:, :, lo:hi].rearrange("p j (c i) -> p c j i", i=4),
+                    in_=rows_of[b][z][:, :, lo:hi].rearrange("p j (c i) -> p c j i", i=4),
                 )
             for z, lo, hi in pieces:
                 nc.vector.quantize_mx(
@@ -90,7 +92,7 @@ def tile_picked_widxput_gate_l_kernel(tc, x_words, x_scales, mem, w1, slot, out)
         nc.sync.dma_start(out=raw[1][0][:], in_=w_rows(1, 0))
         nc.sync.dma_start(offsets[:], slot)
         nc.sync.dma_start(out=store[0][:], in_=mem[0:P, :])
-        nc.sync.dma_start(out=raw[1][1][:], in_=w_rows(1, 1))
+        nc.sync.dma_start(out=rows_of[1][1], in_=w_rows(1, 1))
         nc.sync.dma_start(out=store[1][:], in_=mem[P : 2 * P, :])
 
         quantise(0, [(0, 0, P)])

from contextlib import ExitStack

import concourse.mybir as mybir

K, T, N, U = 1024, 512, 256, 1024
FLOPS = 2 * K * T * N

F32 = mybir.dt.float32
BF16 = mybir.dt.bfloat16
I32 = mybir.dt.int32
U32 = mybir.dt.uint32
U16 = mybir.dt.uint16
U8 = mybir.dt.uint8
FP8X4 = mybir.dt.float8_e4m3fn_x4
FP4X4 = mybir.dt.float4_e2m1fn_x4
MULT = mybir.AluOpType.mult
SIGMOID = mybir.ActivationFunctionType.Sigmoid
COPY = mybir.ActivationFunctionType.Copy

P = 128
PACK = 4
K_PASS = P * PACK
PASSES = K // K_PASS
HALF = T // 2
FIRST = 128
FUSED = 192
AXI = 256


def tile_picked_widxput_gate_l_kernel(tc, x_words, x_scales, mem, w1, slot, out):
    nc = tc.nc
    with ExitStack() as ctx:
        keep = ctx.enter_context(tc.tile_pool(name="keep", bufs=1))
        psum = ctx.enter_context(tc.psum_pool(name="psum", bufs=1))

        offsets = keep.tile([P, T // 16], U16, name="offsets", align_bytes=AXI)
        xw = keep.tile([P, PASSES, 2 * T], U8, name="xw", align_bytes=AXI)
        xs = keep.tile([P, PASSES, T], U8, name="xs", align_bytes=AXI)
        raw = [[keep.tile([P, PACK, P], F32, name=f"raw{b}{z}", align_bytes=AXI) for z in range(PASSES - b)] for b in range(2)]
        wide = keep.tile([P, PACK, N], F32, name="wide", align_bytes=AXI)
        rows_of = [[raw[0][0][:], raw[0][1][:]], [raw[1][0][:], wide[:, :, 0:P]]]
        late = keep.tile([P, T], F32, name="late", align_bytes=64)
        woven = [keep.tile([P, K_PASS], BF16, name=f"woven{i}", align_bytes=64) for i in range(3)]
        grouped = [[woven[0][:], woven[1][:]], [woven[2][:], late[:, FUSED : FUSED + HALF].bitcast(BF16)]]
        codes = [[keep.tile([P, P], U32, name=f"codes{b}{z}", align_bytes=64) for z in range(PASSES)] for b in range(2)]
        scales = [[keep.tile([P, P], U8, name=f"scales{b}{z}", align_bytes=64) for z in range(PASSES)] for b in range(2)]
        store = [keep.tile([P, U], F32, name=f"store{b}", align_bytes=AXI) for b in range(2)]
        gate = [keep.tile([P, T], F32, name=f"gate{b}") for b in range(2)]
        old0 = keep.tile([P, T], F32, name="old0")
        old1 = keep.tile([P, T], F32, name="old1")
        banks = [psum.tile([P, T], F32, name=f"bank{i}") for i in range(8)]

        def w_rows(b, z):
            rows = w1[z * K_PASS : (z + 1) * K_PASS, b * P : (b + 1) * P]
            return rows.rearrange("(p j) m -> p j m", j=PACK)

        def listed(b, lo, hi):
            return store[b][:].indirect(offsets[:, lo // 16 : hi // 16])

        def quantise(b, pieces):
            for z, lo, hi in pieces:
                nc.vector.tensor_copy(
                    out=grouped[b][z][:, PACK * lo : PACK * hi].rearrange("p (c i j) -> p c j i", i=4, j=PACK),
                    in_=rows_of[b][z][:, :, lo:hi].rearrange("p j (c i) -> p c j i", i=4),
                )
            for z, lo, hi in pieces:
                nc.vector.quantize_mx(
                    out=codes[b][z][:, lo:hi].bitcast(FP8X4),
                    scales=scales[b][z][:, lo:hi],
                    in_=grouped[b][z][:, PACK * lo : PACK * hi],
                )

        def gates(b, lo, hi, bank):
            for z in range(PASSES):
                nc.tensor.matmul_mx(
                    out=bank[:, lo:hi],
                    lhsT=codes[b][z][:].bitcast(FP8X4),
                    lhsT_scale=scales[b][z][:],
                    rhs=xw[:, z, 2 * lo : 2 * hi].bitcast(FP4X4),
                    rhs_scale=xs[:, z, lo:hi],
                    start=(z == 0),
                    stop=(z == PASSES - 1),
                )
            nc.scalar.activation(out=gate[b][:, lo:hi], in_=bank[:, lo:hi], func=SIGMOID)

        scale_rows = x_scales.rearrange("z (q r) c -> r q z c", r=4)
        for z in range(PASSES):
            nc.sync.dma_start(out=raw[0][z][:], in_=w_rows(0, z))
            for r in (2 * z, 2 * z + 1):
                nc.sync.dma_start(out=xs[r:P:32, :, :].bitcast(I32), in_=scale_rows[r].bitcast(I32))
        nc.sync.dma_start(out=xw[:].bitcast(I32), in_=x_words.rearrange("z p c -> p z c").bitcast(I32))
        nc.sync.dma_start(out=raw[1][0][:], in_=w_rows(1, 0))
        nc.sync.dma_start(offsets[:], slot)
        nc.sync.dma_start(out=store[0][:], in_=mem[0:P, :])
        nc.sync.dma_start(out=rows_of[1][1], in_=w_rows(1, 1))
        nc.sync.dma_start(out=store[1][:], in_=mem[P : 2 * P, :])

        quantise(0, [(0, 0, P)])
        quantise(0, [(1, 0, P // 2), (1, P // 2, P)])
        for g in range(T // P):
            gates(0, g * P, (g + 1) * P, banks[g])
        quantise(1, [(0, 0, P)])
        nc.vector.tensor_tensor(late[:, 0:FUSED], listed(0, 0, FUSED), gate[0][:, 0:FUSED], MULT)
        nc.scalar.activation(old0[:, FUSED:T], listed(0, FUSED, T), COPY)
        nc.scalar.activation(listed(0, 0, FIRST), late[:, 0:FIRST], COPY)
        quantise(1, [(1, 0, P // 2), (1, P // 2, P)])
        for g in range(T // P):
            gates(1, g * P, (g + 1) * P, banks[4 + g])
        nc.vector.tensor_copy(old1[:], listed(1, 0, T))
        nc.gpsimd.tensor_tensor(late[:, FUSED:T], old0[:, FUSED:T], gate[0][:, FUSED:T], MULT)
        nc.scalar.activation(listed(0, FIRST, T), late[:, FIRST:T], COPY)
        nc.sync.dma_start(out=out[0:P, :], in_=store[0][:])
        nc.vector.tensor_tensor(listed(1, 0, T), old1[:], gate[1][:], MULT)
        nc.sync.dma_start(out=out[P : 2 * P, :], in_=store[1][:])
